import numpy as np
CORES = [4,5,6,7,0,1,2,3]
N = 8
ROOT = 3
WIDTHS = [16,48,4,96,8,64,32,24]
OFF = [0,16,64,68,164,172,236,268]
C = 292
def setup_inputs(rng):
    return {"x": rng.standard_normal((N, 128, C), dtype=np.float32)}
def reference(x):
    YW = max(WIDTHS)
    y = np.full((N, 128, YW), np.nan, x.dtype)
    for r in range(N):
        y[r][:, :WIDTHS[r]] = x[ROOT][:, OFF[r]:OFF[r] + WIDTHS[r]]
    return {"y": y}

SCRATCH = {
    "stage": ("sbuf", [128, 292], "float32"),
    "land": ("sbuf", [128, 96], "float32"),
}
SEMAPHORES = ["loaded", "read", "arrived", "stored"]

ENGINES = 16


def rank_program(g, core, T, topo):
    rank = T.rank_of(core)
    if rank is None:
        return

    widths = T.tables["WIDTHS"]
    off = T.tables["OFF"]
    total = T.tables["C"]
    root = T.root
    width = widths[rank]

    if rank != root:
        g.wait_ge(T.sem.arrived, ENGINES)
        g.dma_start(T.y[:, 0:width], T.land[:, 0:width]).then_inc(T.sem.stored, 16)
        g.wait_ge(T.sem.stored, 16)
        return

    lo, hi = off[root], off[root] + width
    loads = 0
    for a, b in ((0, lo), (hi, total)):
        if b > a:
            g.dma_start(T.stage[:, a:b], T.x[:, a:b]).then_inc(T.sem.loaded, 16)
            loads += 1
    g.dma_start(T.y[:, 0:width], T.x[:, lo:hi]).then_inc(T.sem.stored, 16)

    g.wait_ge(T.sem.loaded, 16 * loads)

    sends = 0
    for r in range(len(T.cores)):
        if r == root:
            continue
        dst = T.cores[r]
        rid, pid = topo.addr(dst)[0:2]
        g.remote_dma(
            T.land[:, 0:widths[r]],
            T.stage[:, off[r]:off[r] + widths[r]],
            remote_sem=T.sem.arrived,
            local_sem=T.sem.read,
            pid=pid,
            routing_id=rid,
            dma_engine_mask=topo.mask(core, dst),
        )
        sends += 1

    g.wait_ge(T.sem.read, ENGINES * sends)
    g.wait_ge(T.sem.stored, 16)
